import numpy as np
import ml_dtypes


def mxq(x, axis, fmt="e4m3"):
    dtype, down = {"e4m3": (ml_dtypes.float8_e4m3fn, 7), "e5m2": (ml_dtypes.float8_e5m2, 14)}[fmt]
    v = np.moveaxis(np.asarray(x, np.float32).astype(ml_dtypes.bfloat16).astype(np.float64), axis, -1)
    blocks = v.reshape(v.shape[:-1] + (-1, 32))
    amax = np.abs(blocks).max(-1, keepdims=True)
    byte = np.maximum(np.where(amax > 0, np.frexp(amax)[1] - 1 + 127, 0) - down, 1)
    scale = np.exp2(byte - 127.0)
    codes = (blocks / scale).astype(np.float32).astype(dtype).astype(np.float64)
    return np.moveaxis((codes * scale).reshape(v.shape), -1, axis)


WIDE = False


def mx_kscale(k):
    if not WIDE:
        return np.ones(k)
    levels = np.array([18, -18])
    if k % 512:
        return np.exp2(np.random.permutation(np.resize(levels, k // 32))).repeat(32)
    a = np.empty((k // 512, 16))
    for p in range(k // 512):
        a[p, :8] = np.random.permutation(np.resize(levels, 8))
        for g in range(8):
            far = levels[np.abs(levels - a[p, g]) >= 10]
            a[p, g + 8] = far[np.random.randint(len(far))]
    return np.exp2(a.ravel()).repeat(32)


def f64(x):
    return np.asarray(x).astype(np.float64)


def striped(idx):
    return np.tile(np.asarray(idx).reshape(-1, 16).T, (8, 1)).astype(np.uint16)


def unstriped(offs):
    return offs[:16].T.reshape(-1).astype(np.int64)


B, N, T, D, DV, NQ = 1, 1024, 2048, 512, 512, 256
PAGE = 128


def setup_inputs():
    n = np.random.standard_normal
    pages = np.random.permutation(T // PAGE)[:B * N // PAGE]
    idx = (pages[:, None] * PAGE + np.arange(PAGE)[None, :]).reshape(-1)
    u = mx_kscale(B * N)
    ut = np.ones(T)
    ut[idx] = u
    w = np.exp(n((B, N, NQ)))
    w = w / w.sum(1, keepdims=True)
    return {
        "wT": (w * u.reshape(B, N, 1)).astype(np.float32),
        "vT": (n((DV, T)) / ut).astype(np.float32),
        "offs": striped(idx),
    }


def reference(wT, vT, offs):
    idx = unstriped(offs)
    pick = lambda x: x[:, idx].reshape(x.shape[0], B, N).transpose(1, 0, 2)
    return mxq(f64(wT), 1, "e5m2").transpose(0, 2, 1) @ mxq(pick(f64(vT)).transpose(0, 2, 1), 1, "e4m3")

@@ -1,0 +1,132 @@
+from contextlib import ExitStack
+
+import concourse.mybir as mybir
+from concourse.masks import make_identity
+
+P = 128
+SLOTS, QUERIES, TOKENS, FEATURES = 1024, 256, 2048, 512
+PASS = 512
+PASSES = SLOTS // PASS
+BLOCKS = FEATURES // P
+QBLOCKS = QUERIES // P
+FLOPS = 2 * SLOTS * QUERIES * FEATURES
+
+F32 = mybir.dt.float32
+BF16 = mybir.dt.bfloat16
+U32 = mybir.dt.uint32
+U16 = mybir.dt.uint16
+U8 = mybir.dt.uint8
+E4M3 = mybir.dt.float8_e4m3fn_x4
+E5M2 = mybir.dt.float8_e5m2_x4
+
+
+def tile_attend_spmm_kernel(tc, wT, vT, offs, out):
+    nc = tc.nc
+    with ExitStack() as ctx:
+        held = ctx.enter_context(tc.tile_pool(name="held", bufs=1))
+        ring = ctx.enter_context(tc.tile_pool(name="ring", bufs=4))
+        turned_pool = ctx.enter_context(tc.psum_pool(name="turned_pool", bufs=4))
+        sums_pool = ctx.enter_context(tc.psum_pool(name="sums_pool", bufs=1))
+
+        offsets = held.tile([P, SLOTS // 16], U16, name="offsets")
+        nc.sync.dma_start(offsets[:], offs)
+
+        pool_tiles = [held.tile([P, TOKENS], F32, name=f"values{f}") for f in range(BLOCKS)]
+        w_raw = [held.tile([P, 4, QUERIES], F32, name=f"w_raw{g}") for g in range(PASSES)]
+
+        def load_values(f):
+            nc.sync.dma_start(pool_tiles[f][:], vT[f * P : (f + 1) * P, :])
+
+        def load_weights(g):
+            rows = wT[0, g * PASS : (g + 1) * PASS, :]
+            nc.sync.dma_start(w_raw[g][:], rows.rearrange("(p j) q -> p j q", j=4))
+
+        load_values(0)
+        load_weights(0)
+        load_values(1)
+        load_values(2)
+        load_values(3)
+        load_weights(1)
+
+        ident = held.tile([P, P], F32, name="ident")
+        make_identity(nc, ident[:])
+
+        w_codes = [held.tile([P, QUERIES], U32, name=f"w_codes{g}", align_bytes=64) for g in range(PASSES)]
+        w_scales = [held.tile([P, QUERIES], U8, name=f"w_scales{g}", align_bytes=64) for g in range(PASSES)]
+        v_codes = [held.tile([P, FEATURES], U32, name=f"v_codes{g}", align_bytes=64) for g in range(PASSES)]
+        v_scales = [held.tile([P, FEATURES], U8, name=f"v_scales{g}", align_bytes=64) for g in range(PASSES)]
+        w_grouped = [held.tile([P, QUERIES, 4], BF16, name=f"w_grouped{g}", align_bytes=64) for g in range(PASSES)]
+        sums = [sums_pool.tile([P, FEATURES], F32, name=f"sums{b}") for b in range(QBLOCKS)]
+
+        def gather(f, g):
+            picked = ring.tile([P, 2, P, 2], BF16, name="picked", align_bytes=64)
+            nc.vector.tensor_copy(
+                picked[:].rearrange("p u s e -> p s u e"),
+                pool_tiles[f][:].indirect(offsets[:, g * (PASS // 16) : (g + 1) * (PASS // 16)]),
+            )
+            return picked
+
+        def turn(picked):
+            words = picked[:].rearrange("p u s e -> p (u s e)").bitcast(F32)
+            turned = turned_pool.tile([P, 2, P], F32, name="turned")
+            for u in range(2):
+                nc.tensor.transpose(turned[:, u, :], words[:, u * P : (u + 1) * P], ident[:])
+            grouped = ring.tile([P, P, 4], BF16, name="grouped", align_bytes=64)
+            nc.scalar.copy(
+                grouped[:].rearrange("s f t -> s (f t)").bitcast(F32).rearrange("s (f u) -> s f u", u=2),
+                turned[:].rearrange("s u f -> s f u"),
+            )
+            return grouped
+
+        def quantise_values(grouped, f, g):
+            cols = slice(f * P, (f + 1) * P)
+            nc.vector.quantize_mx(
+                out=v_codes[g][:, cols].bitcast(E4M3),
+                scales=v_scales[g][:, cols],
+                in_=grouped[:].rearrange("s f t -> s (f t)"),
+            )
+
+        def group_weights(g, engine_copy):
+            engine_copy(w_grouped[g][:], w_raw[g][:].rearrange("p j q -> p q j"))
+
+        def quantise_weights(g):
+            nc.vector.quantize_mx(
+                out=w_codes[g][:].bitcast(E5M2),
+                scales=w_scales[g][:],
+                in_=w_grouped[g][:].rearrange("p q j -> p (q j)"),
+            )
+
+        def multiply(g):
+            for b in range(QBLOCKS):
+                queries = slice(b * P, (b + 1) * P)
+                nc.tensor.matmul_mx(
+                    out=sums[b][:],
+                    lhsT=w_codes[g][:, queries].bitcast(E5M2),
+                    lhsT_scale=w_scales[g][:, queries],
+                    rhs=v_codes[g][:].bitcast(E4M3),
+                    rhs_scale=v_scales[g][:],
+                    start=(g == 0),
+                    stop=(g == PASSES - 1),
+                )
+
+        waiting = None
+        for f in range(BLOCKS):
+            for g in range(PASSES):
+                picked = gather(f, g)
+                if waiting is not None:
+                    quantise_values(*waiting)
+                waiting = (turn(picked), f, g)
+            if f == 0:
+                group_weights(0, nc.scalar.copy)
+            if f == 1:
+                quantise_weights(0)
+        group_weights(1, nc.vector.tensor_copy)
+        quantise_values(*waiting)
+        quantise_weights(1)
+        multiply(0)
+        multiply(1)
+
+        for b in range(QBLOCKS):
+            result = held.tile([P, FEATURES], F32, name=f"result{b}")
+            (nc.vector.tensor_copy if b == 0 else nc.scalar.copy)(result[:], sums[b][:])
+            nc.sync.dma_start(out[0, b * P : (b + 1) * P, :], result[:])

@@ -42,9 +42,9 @@ def tile_attend_spmm_kernel(tc, wT, vT, offs, out):
             nc.sync.dma_start(w_raw[g][:], rows.rearrange("(p j) q -> p j q", j=4))
 
         load_values(0)
-        load_weights(0)
         load_values(1)
         load_values(2)
+        load_weights(0)
         load_values(3)
         load_weights(1)
 
@@ -58,13 +58,16 @@ def tile_attend_spmm_kernel(tc, wT, vT, offs, out):
         w_grouped = [held.tile([P, QUERIES, 4], BF16, name=f"w_grouped{g}", align_bytes=64) for g in range(PASSES)]
         sums = [sums_pool.tile([P, FEATURES], F32, name=f"sums{b}") for b in range(QBLOCKS)]
 
-        def gather(f, g):
+        def gather(engine_copy, table, g):
             picked = ring.tile([P, 2, P, 2], BF16, name="picked", align_bytes=64)
-            nc.vector.tensor_copy(
+            engine_copy(
                 picked[:].rearrange("p u s e -> p s u e"),
-                pool_tiles[f][:].indirect(offsets[:, g * (PASS // 16) : (g + 1) * (PASS // 16)]),
+                table[:].indirect(offsets[:, g * (PASS // 16) : (g + 1) * (PASS // 16)]),
             )
             return picked
+
+        def scalar_copy(dst, src):
+            nc.scalar.activation(dst, src, mybir.ActivationFunctionType.Copy)
 
         def turn(picked):
             words = picked[:].rearrange("p u s e -> p (u s e)").bitcast(F32)
@@ -109,21 +112,39 @@ def tile_attend_spmm_kernel(tc, wT, vT, offs, out):
                     stop=(g == PASSES - 1),
                 )
 
-        waiting = None
-        for f in range(BLOCKS):
-            for g in range(PASSES):
-                picked = gather(f, g)
-                if waiting is not None:
-                    quantise_values(*waiting)
-                waiting = (turn(picked), f, g)
-            if f == 0:
-                group_weights(0, nc.scalar.copy)
-            if f == 1:
-                quantise_weights(0)
-        group_weights(1, nc.vector.tensor_copy)
-        quantise_values(*waiting)
-        quantise_weights(1)
+        vector_copy = nc.vector.tensor_copy
+        half = held.tile([P, TOKENS], BF16, name="half")
+
+        p00 = gather(vector_copy, pool_tiles[0], 0)
+        g00 = turn(p00)
+        p01 = gather(vector_copy, pool_tiles[0], 1)
+        g01 = turn(p01)
+        vector_copy(half[:], pool_tiles[1][:])
+        p10 = gather(scalar_copy, half, 0)
+        p11 = gather(scalar_copy, half, 1)
+        quantise_values(g00, 0, 0)
+        quantise_values(g01, 0, 1)
+        p20 = gather(vector_copy, pool_tiles[2], 0)
+        g10 = turn(p10)
+        g11 = turn(p11)
+        p21 = gather(vector_copy, pool_tiles[2], 1)
+        quantise_values(g10, 1, 0)
+        quantise_values(g11, 1, 1)
+        g20 = turn(p20)
+        group_weights(0, nc.scalar.copy)
+        g21 = turn(p21)
+        p30 = gather(vector_copy, pool_tiles[3], 0)
+        quantise_values(g20, 2, 0)
+        g30 = turn(p30)
+        p31 = gather(vector_copy, pool_tiles[3], 1)
+        quantise_weights(0)
+        quantise_values(g21, 2, 1)
+        group_weights(1, nc.scalar.copy)
+        quantise_values(g30, 3, 0)
+        g31 = turn(p31)
         multiply(0)
+        quantise_weights(1)
+        quantise_values(g31, 3, 1)
         multiply(1)
 
         for b in range(QBLOCKS):

@@ -24,29 +24,28 @@ def tile_attend_spmm_kernel(tc, wT, vT, offs, out):
     nc = tc.nc
     with ExitStack() as ctx:
         held = ctx.enter_context(tc.tile_pool(name="held", bufs=1))
-        ring = ctx.enter_context(tc.tile_pool(name="ring", bufs=4))
-        turned_pool = ctx.enter_context(tc.psum_pool(name="turned_pool", bufs=4))
+        ring = ctx.enter_context(tc.tile_pool(name="ring", bufs=8))
+        turned_pool = ctx.enter_context(tc.psum_pool(name="turned_pool", bufs=6))
         sums_pool = ctx.enter_context(tc.psum_pool(name="sums_pool", bufs=1))
 
         offsets = held.tile([P, SLOTS // 16], U16, name="offsets")
-        nc.sync.dma_start(offsets[:], offs)
 
         pool_tiles = [held.tile([P, TOKENS], F32, name=f"values{f}") for f in range(BLOCKS)]
         w_raw = [held.tile([P, 4, QUERIES], F32, name=f"w_raw{g}") for g in range(PASSES)]
 
-        def load_values(f):
-            nc.sync.dma_start(pool_tiles[f][:], vT[f * P : (f + 1) * P, :])
+        def load_weights(g, first, last):
+            rows = wT[0, g * PASS : (g + 1) * PASS, first:last]
+            nc.sync.dma_start(w_raw[g][:, :, first:last], rows.rearrange("(p j) q -> p j q", j=4))
 
-        def load_weights(g):
-            rows = wT[0, g * PASS : (g + 1) * PASS, :]
-            nc.sync.dma_start(w_raw[g][:], rows.rearrange("(p j) q -> p j q", j=4))
-
-        load_values(0)
-        load_values(1)
-        load_values(2)
-        load_weights(0)
-        load_values(3)
-        load_weights(1)
+        nc.sync.dma_start(pool_tiles[0][:], vT[0 * P : 1 * P, :])
+        nc.sync.dma_start(offsets[:], offs)
+        nc.sync.dma_start(pool_tiles[1][:], vT[1 * P : 2 * P, :])
+        nc.sync.dma_start(pool_tiles[2][:], vT[2 * P : 3 * P, :])
+        nc.sync.dma_start(pool_tiles[3][:], vT[3 * P : 4 * P, :])
+        load_weights(0, 0, P)
+        load_weights(0, P, QUERIES)
+        load_weights(1, 0, P)
+        load_weights(1, P, QUERIES)
 
         ident = held.tile([P, P], F32, name="ident")
         make_identity(nc, ident[:])
@@ -74,8 +73,11 @@ def tile_attend_spmm_kernel(tc, wT, vT, offs, out):
             turned = turned_pool.tile([P, 2, P], F32, name="turned")
             for u in range(2):
                 nc.tensor.transpose(turned[:, u, :], words[:, u * P : (u + 1) * P], ident[:])
+            return turned
+
+        def empty(engine_copy, turned):
             grouped = ring.tile([P, P, 4], BF16, name="grouped", align_bytes=64)
-            nc.scalar.copy(
+            engine_copy(
                 grouped[:].rearrange("s f t -> s (f t)").bitcast(F32).rearrange("s (f u) -> s f u", u=2),
                 turned[:].rearrange("s u f -> s f u"),
             )
@@ -89,65 +91,83 @@ def tile_attend_spmm_kernel(tc, wT, vT, offs, out):
                 in_=grouped[:].rearrange("s f t -> s (f t)"),
             )
 
-        def group_weights(g, engine_copy):
-            engine_copy(w_grouped[g][:], w_raw[g][:].rearrange("p j q -> p q j"))
+        def group_weights(engine_copy, g, first, last):
+            engine_copy(w_grouped[g][:, first:last, :], w_raw[g][:, :, first:last].rearrange("p j q -> p q j"))
 
-        def quantise_weights(g):
+        def quantise_weights(g, first, last):
             nc.vector.quantize_mx(
-                out=w_codes[g][:].bitcast(E5M2),
-                scales=w_scales[g][:],
-                in_=w_grouped[g][:].rearrange("p q j -> p (q j)"),
+                out=w_codes[g][:, first:last].bitcast(E5M2),
+                scales=w_scales[g][:, first:last],
+                in_=w_grouped[g][:, first:last, :].rearrange("p q j -> p (q j)"),
             )
 
-        def multiply(g):
-            for b in range(QBLOCKS):
-                queries = slice(b * P, (b + 1) * P)
-                nc.tensor.matmul_mx(
-                    out=sums[b][:],
-                    lhsT=w_codes[g][:, queries].bitcast(E5M2),
-                    lhsT_scale=w_scales[g][:, queries],
-                    rhs=v_codes[g][:].bitcast(E4M3),
-                    rhs_scale=v_scales[g][:],
-                    start=(g == 0),
-                    stop=(g == PASSES - 1),
-                )
+        def multiply(g, b):
+            queries = slice(b * P, (b + 1) * P)
+            nc.tensor.matmul_mx(
+                out=sums[b][:],
+                lhsT=w_codes[g][:, queries].bitcast(E5M2),
+                lhsT_scale=w_scales[g][:, queries],
+                rhs=v_codes[g][:].bitcast(E4M3),
+                rhs_scale=v_scales[g][:],
+                start=(g == 0),
+                stop=(g == PASSES - 1),
+            )
+
+        def finish(engine_copy, b):
+            result = held.tile([P, FEATURES], F32, name=f"result{b}")
+            engine_copy(result[:], sums[b][:])
+            nc.sync.dma_start(out[0, b * P : (b + 1) * P, :], result[:])
 
         vector_copy = nc.vector.tensor_copy
-        half = held.tile([P, TOKENS], BF16, name="half")
-
-        p00 = gather(vector_copy, pool_tiles[0], 0)
-        g00 = turn(p00)
+        half0 = held.tile([P, TOKENS], BF16, name="half0")
+        half1 = held.tile([P, TOKENS], BF16, name="half1")
+        vector_copy(half0[:, 0:1536], pool_tiles[0][:, 0:1536])
+        scalar_copy(half0[:, 1536:TOKENS], pool_tiles[0][:, 1536:TOKENS])
         p01 = gather(vector_copy, pool_tiles[0], 1)
-        g01 = turn(p01)
-        vector_copy(half[:], pool_tiles[1][:])
-        p10 = gather(scalar_copy, half, 0)
-        p11 = gather(scalar_copy, half, 1)
-        quantise_values(g00, 0, 0)
+        p00 = gather(scalar_copy, half0, 0)
+        vector_copy(half1[:, 0:1024], pool_tiles[1][:, 0:1024])
+        scalar_copy(half1[:, 1024:TOKENS], pool_tiles[1][:, 1024:TOKENS])
+        t01 = turn(p01)
+        t00 = turn(p00)
+        g01 = empty(vector_copy, t01)
+        g00 = empty(vector_copy, t00)
+        p10 = gather(scalar_copy, half1, 0)
         quantise_values(g01, 0, 1)
+        quantise_values(g00, 0, 0)
         p20 = gather(vector_copy, pool_tiles[2], 0)
-        g10 = turn(p10)
-        g11 = turn(p11)
+        p11 = gather(scalar_copy, half1, 1)
+        t10 = turn(p10)
         p21 = gather(vector_copy, pool_tiles[2], 1)
-        quantise_values(g10, 1, 0)
-        quantise_values(g11, 1, 1)
-        g20 = turn(p20)
-        group_weights(0, nc.scalar.copy)
-        g21 = turn(p21)
+        t20 = turn(p20)
+        t11 = turn(p11)
+        g20 = empty(nc.scalar.copy, t20)
+        g10 = empty(nc.scalar.copy, t10)
+        t21 = turn(p21)
         p30 = gather(vector_copy, pool_tiles[3], 0)
+        g11 = empty(nc.scalar.copy, t11)
+        g21 = empty(nc.scalar.copy, t21)
+        quantise_values(g11, 1, 1)
         quantise_values(g20, 2, 0)
-        g30 = turn(p30)
+        group_weights(nc.scalar.copy, 0, 0, P)
+        t30 = turn(p30)
         p31 = gather(vector_copy, pool_tiles[3], 1)
-        quantise_weights(0)
-        quantise_values(g21, 2, 1)
-        group_weights(1, nc.scalar.copy)
+        g30 = empty(nc.scalar.copy, t30)
+        group_weights(nc.scalar.copy, 0, P, QUERIES)
         quantise_values(g30, 3, 0)
-        g31 = turn(p31)
-        multiply(0)
-        quantise_weights(1)
+        t31 = turn(p31)
+        quantise_values(g10, 1, 0)
+        quantise_weights(0, 0, P)
+        group_weights(nc.scalar.copy, 1, 0, P)
+        quantise_values(g21, 2, 1)
+        quantise_weights(0, P, QUERIES)
+        multiply(0, 0)
+        g31 = empty(vector_copy, t31)
+        multiply(0, 1)
+        group_weights(nc.scalar.copy, 1, P, QUERIES)
+        quantise_weights(1, 0, P)
         quantise_values(g31, 3, 1)
-        multiply(1)
-
-        for b in range(QBLOCKS):
-            result = held.tile([P, FEATURES], F32, name=f"result{b}")
-            (nc.vector.tensor_copy if b == 0 else nc.scalar.copy)(result[:], sums[b][:])
-            nc.sync.dma_start(out[0, b * P : (b + 1) * P, :], result[:])
+        quantise_weights(1, P, QUERIES)
+        multiply(1, 0)
+        multiply(1, 1)
+        finish(vector_copy, 0)
+        finish(nc.scalar.copy, 1)

@@ -37,10 +37,10 @@ def tile_attend_spmm_kernel(tc, wT, vT, offs, out):
             rows = wT[0, g * PASS : (g + 1) * PASS, first:last]
             nc.sync.dma_start(w_raw[g][:, :, first:last], rows.rearrange("(p j) q -> p j q", j=4))
 
-        nc.sync.dma_start(pool_tiles[0][:], vT[0 * P : 1 * P, :])
         nc.sync.dma_start(offsets[:], offs)
-        nc.sync.dma_start(pool_tiles[1][:], vT[1 * P : 2 * P, :])
+        nc.sync.dma_start(pool_tiles[0][:], vT[0 * P : 1 * P, :])
         nc.sync.dma_start(pool_tiles[2][:], vT[2 * P : 3 * P, :])
+        nc.sync.dma_start(pool_tiles[1][:], vT[1 * P : 2 * P, :])
         nc.sync.dma_start(pool_tiles[3][:], vT[3 * P : 4 * P, :])
         load_weights(0, 0, P)
         load_weights(0, P, QUERIES)
@@ -113,61 +113,67 @@ def tile_attend_spmm_kernel(tc, wT, vT, offs, out):
                 stop=(g == PASSES - 1),
             )
 
-        def finish(engine_copy, b):
-            result = held.tile([P, FEATURES], F32, name=f"result{b}")
-            engine_copy(result[:], sums[b][:])
-            nc.sync.dma_start(out[0, b * P : (b + 1) * P, :], result[:])
+        def finish(engine_copy, result, b, first, last):
+            engine_copy(result[:, first:last], sums[b][:, first:last])
+            nc.sync.dma_start(out[0, b * P : (b + 1) * P, first:last], result[:, first:last])
+
+        def gpsimd_copy(dst, src):
+            nc.gpsimd.tensor_scalar(dst, src, 1.0, 0.0, mybir.AluOpType.mult, mybir.AluOpType.add)
 
         vector_copy = nc.vector.tensor_copy
         half0 = held.tile([P, TOKENS], BF16, name="half0")
         half1 = held.tile([P, TOKENS], BF16, name="half1")
+        result0 = held.tile([P, FEATURES], F32, name="result0")
+        result1 = held.tile([P, FEATURES], F32, name="result1")
         vector_copy(half0[:, 0:1536], pool_tiles[0][:, 0:1536])
         scalar_copy(half0[:, 1536:TOKENS], pool_tiles[0][:, 1536:TOKENS])
-        p01 = gather(vector_copy, pool_tiles[0], 1)
-        p00 = gather(scalar_copy, half0, 0)
-        vector_copy(half1[:, 0:1024], pool_tiles[1][:, 0:1024])
-        scalar_copy(half1[:, 1024:TOKENS], pool_tiles[1][:, 1024:TOKENS])
-        t01 = turn(p01)
+        p00 = gather(vector_copy, pool_tiles[0], 0)
+        p01 = gather(scalar_copy, half0, 1)
+        p21 = gather(vector_copy, pool_tiles[2], 1)
         t00 = turn(p00)
-        g01 = empty(vector_copy, t01)
-        g00 = empty(vector_copy, t00)
-        p10 = gather(scalar_copy, half1, 0)
-        quantise_values(g01, 0, 1)
-        quantise_values(g00, 0, 0)
+        t01 = turn(p01)
+        g00 = empty(nc.scalar.copy, t00)
         p20 = gather(vector_copy, pool_tiles[2], 0)
+        g01 = empty(nc.scalar.copy, t01)
+        t21 = turn(p21)
+        g21 = empty(nc.scalar.copy, t21)
+        quantise_values(g00, 0, 0)
+        scalar_copy(half1[:, 1536:TOKENS], pool_tiles[1][:, 1536:TOKENS])
+        t20 = turn(p20)
+        quantise_values(g21, 2, 1)
+        vector_copy(half1[:, 0:1536], pool_tiles[1][:, 0:1536])
+        g20 = empty(nc.scalar.copy, t20)
+        quantise_values(g01, 0, 1)
+        p10 = gather(scalar_copy, half1, 0)
+        quantise_values(g20, 2, 0)
+        p30 = gather(vector_copy, pool_tiles[3], 0)
+        group_weights(gpsimd_copy, 0, 0, P)
         p11 = gather(scalar_copy, half1, 1)
         t10 = turn(p10)
-        p21 = gather(vector_copy, pool_tiles[2], 1)
-        t20 = turn(p20)
-        t11 = turn(p11)
-        g20 = empty(nc.scalar.copy, t20)
-        g10 = empty(nc.scalar.copy, t10)
-        t21 = turn(p21)
-        p30 = gather(vector_copy, pool_tiles[3], 0)
-        g11 = empty(nc.scalar.copy, t11)
-        g21 = empty(nc.scalar.copy, t21)
-        quantise_values(g11, 1, 1)
-        quantise_values(g20, 2, 0)
-        group_weights(nc.scalar.copy, 0, 0, P)
-        t30 = turn(p30)
         p31 = gather(vector_copy, pool_tiles[3], 1)
+        t30 = turn(p30)
+        group_weights(gpsimd_copy, 0, P, QUERIES)
+        g10 = empty(vector_copy, t10)
         g30 = empty(nc.scalar.copy, t30)
-        group_weights(nc.scalar.copy, 0, P, QUERIES)
-        quantise_values(g30, 3, 0)
         t31 = turn(p31)
-        quantise_values(g10, 1, 0)
+        group_weights(gpsimd_copy, 1, 0, P)
         quantise_weights(0, 0, P)
-        group_weights(nc.scalar.copy, 1, 0, P)
-        quantise_values(g21, 2, 1)
+        t11 = turn(p11)
+        quantise_values(g10, 1, 0)
+        g31 = empty(nc.scalar.copy, t31)
+        quantise_values(g30, 3, 0)
         quantise_weights(0, P, QUERIES)
         multiply(0, 0)
-        g31 = empty(vector_copy, t31)
-        multiply(0, 1)
-        group_weights(nc.scalar.copy, 1, P, QUERIES)
-        quantise_weights(1, 0, P)
+        g11 = empty(nc.scalar.copy, t11)
+        group_weights(gpsimd_copy, 1, P, QUERIES)
         quantise_values(g31, 3, 1)
-        quantise_weights(1, P, QUERIES)
+        quantise_weights(1, 0, P)
+        multiply(0, 1)
+        quantise_values(g11, 1, 1)
         multiply(1, 0)
+        quantise_weights(1, P, QUERIES)
         multiply(1, 1)
-        finish(vector_copy, 0)
-        finish(nc.scalar.copy, 1)
+        finish(nc.scalar.copy, result0, 0, 0, FEATURES // 2)
+        finish(vector_copy, result1, 1, 0, FEATURES // 2)
+        finish(nc.scalar.copy, result0, 0, FEATURES // 2, FEATURES)
+        finish(vector_copy, result1, 1, FEATURES // 2, FEATURES)

@@ -38,10 +38,10 @@ def tile_attend_spmm_kernel(tc, wT, vT, offs, out):
             nc.sync.dma_start(w_raw[g][:, :, first:last], rows.rearrange("(p j) q -> p j q", j=4))
 
         nc.sync.dma_start(offsets[:], offs)
-        nc.sync.dma_start(pool_tiles[0][:], vT[0 * P : 1 * P, :])
-        nc.sync.dma_start(pool_tiles[2][:], vT[2 * P : 3 * P, :])
         nc.sync.dma_start(pool_tiles[1][:], vT[1 * P : 2 * P, :])
+        nc.sync.dma_start(pool_tiles[2][:], vT[2 * P : 3 * P, :])
         nc.sync.dma_start(pool_tiles[3][:], vT[3 * P : 4 * P, :])
+        nc.sync.dma_start(pool_tiles[0][:], vT[0 * P : 1 * P, :])
         load_weights(0, 0, P)
         load_weights(0, P, QUERIES)
         load_weights(1, 0, P)
@@ -75,13 +75,26 @@ def tile_attend_spmm_kernel(tc, wT, vT, offs, out):
                 nc.tensor.transpose(turned[:, u, :], words[:, u * P : (u + 1) * P], ident[:])
             return turned
 
-        def empty(engine_copy, turned):
-            grouped = ring.tile([P, P, 4], BF16, name="grouped", align_bytes=64)
+        pairs = [held.tile([P, 2, P, 4], BF16, name=f"pair{g}", align_bytes=64) for g in range(PASSES)]
+
+        def empty_into(engine_copy, turned, grouped):
             engine_copy(
-                grouped[:].rearrange("s f t -> s (f t)").bitcast(F32).rearrange("s (f u) -> s f u", u=2),
+                grouped.rearrange("s f t -> s (f t)").bitcast(F32).rearrange("s (f u) -> s f u", u=2),
                 turned[:].rearrange("s u f -> s f u"),
             )
+
+        def empty(engine_copy, turned):
+            grouped = ring.tile([P, P, 4], BF16, name="grouped", align_bytes=64)
+            empty_into(engine_copy, turned, grouped[:])
             return grouped
+
+        def quantise_pair(g):
+            cols = slice(0, 2 * P)
+            nc.vector.quantize_mx(
+                out=v_codes[g][:, cols].bitcast(E4M3),
+                scales=v_scales[g][:, cols],
+                in_=pairs[g][:].rearrange("s b f t -> s (b f t)"),
+            )
 
         def quantise_values(grouped, f, g):
             cols = slice(f * P, (f + 1) * P)
@@ -121,59 +134,54 @@ def tile_attend_spmm_kernel(tc, wT, vT, offs, out):
             nc.gpsimd.tensor_scalar(dst, src, 1.0, 0.0, mybir.AluOpType.mult, mybir.AluOpType.add)
 
         vector_copy = nc.vector.tensor_copy
-        half0 = held.tile([P, TOKENS], BF16, name="half0")
-        half1 = held.tile([P, TOKENS], BF16, name="half1")
+        half3 = held.tile([P, TOKENS], BF16, name="half3")
         result0 = held.tile([P, FEATURES], F32, name="result0")
         result1 = held.tile([P, FEATURES], F32, name="result1")
-        vector_copy(half0[:, 0:1536], pool_tiles[0][:, 0:1536])
-        scalar_copy(half0[:, 1536:TOKENS], pool_tiles[0][:, 1536:TOKENS])
-        p00 = gather(vector_copy, pool_tiles[0], 0)
-        p01 = gather(scalar_copy, half0, 1)
-        p21 = gather(vector_copy, pool_tiles[2], 1)
-        t00 = turn(p00)
-        t01 = turn(p01)
-        g00 = empty(nc.scalar.copy, t00)
-        p20 = gather(vector_copy, pool_tiles[2], 0)
-        g01 = empty(nc.scalar.copy, t01)
-        t21 = turn(p21)
-        g21 = empty(nc.scalar.copy, t21)
-        quantise_values(g00, 0, 0)
-        scalar_copy(half1[:, 1536:TOKENS], pool_tiles[1][:, 1536:TOKENS])
-        t20 = turn(p20)
-        quantise_values(g21, 2, 1)
-        vector_copy(half1[:, 0:1536], pool_tiles[1][:, 0:1536])
-        g20 = empty(nc.scalar.copy, t20)
-        quantise_values(g01, 0, 1)
-        p10 = gather(scalar_copy, half1, 0)
-        quantise_values(g20, 2, 0)
-        p30 = gather(vector_copy, pool_tiles[3], 0)
-        group_weights(gpsimd_copy, 0, 0, P)
-        p11 = gather(scalar_copy, half1, 1)
+        p10 = gather(vector_copy, pool_tiles[1], 0)
+        p11 = gather(vector_copy, pool_tiles[1], 1)
         t10 = turn(p10)
-        p31 = gather(vector_copy, pool_tiles[3], 1)
-        t30 = turn(p30)
-        group_weights(gpsimd_copy, 0, P, QUERIES)
-        g10 = empty(vector_copy, t10)
-        g30 = empty(nc.scalar.copy, t30)
-        t31 = turn(p31)
-        group_weights(gpsimd_copy, 1, 0, P)
-        quantise_weights(0, 0, P)
+        p20 = gather(vector_copy, pool_tiles[2], 0)
         t11 = turn(p11)
-        quantise_values(g10, 1, 0)
-        g31 = empty(nc.scalar.copy, t31)
+        empty_into(nc.scalar.copy, t10, pairs[0][:, 1])
+        p21 = gather(vector_copy, pool_tiles[2], 1)
+        t20 = turn(p20)
+        empty_into(nc.scalar.copy, t11, pairs[1][:, 1])
+        scalar_copy(half3[:, 1024:TOKENS], pool_tiles[3][:, 1024:TOKENS])
+        vector_copy(half3[:, 0:1024], pool_tiles[3][:, 0:1024])
+        t21 = turn(p21)
+        p30 = gather(vector_copy, pool_tiles[3], 0)
+        g20 = empty(nc.scalar.copy, t20)
+        g21 = empty(nc.scalar.copy, t21)
+        p00 = gather(vector_copy, pool_tiles[0], 0)
+        t30 = turn(p30)
+        p31 = gather(scalar_copy, half3, 1)
+        quantise_values(g20, 2, 0)
+        t00 = turn(p00)
+        p01 = gather(vector_copy, pool_tiles[0], 1)
+        g30 = empty(nc.scalar.copy, t30)
+        group_weights(nc.scalar.copy, 0, 0, P)
+        t31 = turn(p31)
+        quantise_values(g21, 2, 1)
+        empty_into(nc.scalar.copy, t00, pairs[0][:, 0])
         quantise_values(g30, 3, 0)
+        quantise_weights(0, 0, P)
+        group_weights(nc.scalar.copy, 0, P, QUERIES)
+        t01 = turn(p01)
+        quantise_pair(0)
+        group_weights(nc.scalar.copy, 1, 0, P)
         quantise_weights(0, P, QUERIES)
         multiply(0, 0)
-        g11 = empty(nc.scalar.copy, t11)
-        group_weights(gpsimd_copy, 1, P, QUERIES)
-        quantise_values(g31, 3, 1)
-        quantise_weights(1, 0, P)
+        empty_into(nc.scalar.copy, t01, pairs[1][:, 0])
         multiply(0, 1)
-        quantise_values(g11, 1, 1)
+        quantise_weights(1, 0, P)
+        g31 = empty(nc.scalar.copy, t31)
+        quantise_pair(1)
+        group_weights(nc.scalar.copy, 1, P, QUERIES)
+        quantise_values(g31, 3, 1)
         multiply(1, 0)
         quantise_weights(1, P, QUERIES)
-        multiply(1, 1)
         finish(nc.scalar.copy, result0, 0, 0, FEATURES // 2)
-        finish(vector_copy, result1, 1, 0, FEATURES // 2)
+        multiply(1, 1)
         finish(nc.scalar.copy, result0, 0, FEATURES // 2, FEATURES)
+        finish(vector_copy, result1, 1, 0, FEATURES // 2)
         finish(vector_copy, result1, 1, FEATURES // 2, FEATURES)

from contextlib import ExitStack

import concourse.mybir as mybir
from concourse.masks import make_identity

P = 128
SLOTS, QUERIES, TOKENS, FEATURES = 1024, 256, 2048, 512
PASS = 512
PASSES = SLOTS // PASS
BLOCKS = FEATURES // P
QBLOCKS = QUERIES // P
FLOPS = 2 * SLOTS * QUERIES * FEATURES

F32 = mybir.dt.float32
BF16 = mybir.dt.bfloat16
U32 = mybir.dt.uint32
U16 = mybir.dt.uint16
U8 = mybir.dt.uint8
E4M3 = mybir.dt.float8_e4m3fn_x4
E5M2 = mybir.dt.float8_e5m2_x4


def tile_attend_spmm_kernel(tc, wT, vT, offs, out):
    nc = tc.nc
    with ExitStack() as ctx:
        held = ctx.enter_context(tc.tile_pool(name="held", bufs=1))
        ring = ctx.enter_context(tc.tile_pool(name="ring", bufs=8))
        turned_pool = ctx.enter_context(tc.psum_pool(name="turned_pool", bufs=6))
        sums_pool = ctx.enter_context(tc.psum_pool(name="sums_pool", bufs=1))

        offsets = held.tile([P, SLOTS // 16], U16, name="offsets")

        pool_tiles = [held.tile([P, TOKENS], F32, name=f"values{f}") for f in range(BLOCKS)]
        w_raw = [held.tile([P, 4, QUERIES], F32, name=f"w_raw{g}") for g in range(PASSES)]

        def load_weights(g, first, last):
            rows = wT[0, g * PASS : (g + 1) * PASS, first:last]
            nc.sync.dma_start(w_raw[g][:, :, first:last], rows.rearrange("(p j) q -> p j q", j=4))

        nc.sync.dma_start(offsets[:], offs)
        nc.sync.dma_start(pool_tiles[1][:], vT[1 * P : 2 * P, :])
        nc.sync.dma_start(pool_tiles[2][:], vT[2 * P : 3 * P, :])
        nc.sync.dma_start(pool_tiles[3][:], vT[3 * P : 4 * P, :])
        nc.sync.dma_start(pool_tiles[0][:], vT[0 * P : 1 * P, :])
        load_weights(0, 0, P)
        load_weights(0, P, QUERIES)
        load_weights(1, 0, P)
        load_weights(1, P, QUERIES)

        ident = held.tile([P, P], F32, name="ident")
        make_identity(nc, ident[:])

        w_codes = [held.tile([P, QUERIES], U32, name=f"w_codes{g}", align_bytes=64) for g in range(PASSES)]
        w_scales = [held.tile([P, QUERIES], U8, name=f"w_scales{g}", align_bytes=64) for g in range(PASSES)]
        v_codes = [held.tile([P, FEATURES], U32, name=f"v_codes{g}", align_bytes=64) for g in range(PASSES)]
        v_scales = [held.tile([P, FEATURES], U8, name=f"v_scales{g}", align_bytes=64) for g in range(PASSES)]
        w_grouped = [held.tile([P, QUERIES, 4], BF16, name=f"w_grouped{g}", align_bytes=64) for g in range(PASSES)]
        sums = [sums_pool.tile([P, FEATURES], F32, name=f"sums{b}") for b in range(QBLOCKS)]

        def gather(engine_copy, table, g):
            picked = ring.tile([P, 2, P, 2], BF16, name="picked", align_bytes=64)
            engine_copy(
                picked[:].rearrange("p u s e -> p s u e"),
                table[:].indirect(offsets[:, g * (PASS // 16) : (g + 1) * (PASS // 16)]),
            )
            return picked

        def scalar_copy(dst, src):
            nc.scalar.activation(dst, src, mybir.ActivationFunctionType.Copy)

        def turn(picked):
            words = picked[:].rearrange("p u s e -> p (u s e)").bitcast(F32)
            turned = turned_pool.tile([P, 2, P], F32, name="turned")
            for u in range(2):
                nc.tensor.transpose(turned[:, u, :], words[:, u * P : (u + 1) * P], ident[:])
            return turned

        pairs = [held.tile([P, 2, P, 4], BF16, name=f"pair{g}", align_bytes=64) for g in range(PASSES)]

        def empty_into(engine_copy, turned, grouped):
            engine_copy(
                grouped.rearrange("s f t -> s (f t)").bitcast(F32).rearrange("s (f u) -> s f u", u=2),
                turned[:].rearrange("s u f -> s f u"),
            )

        def empty(engine_copy, turned):
            grouped = ring.tile([P, P, 4], BF16, name="grouped", align_bytes=64)
            empty_into(engine_copy, turned, grouped[:])
            return grouped

        def quantise_pair(g):
            cols = slice(0, 2 * P)
            nc.vector.quantize_mx(
                out=v_codes[g][:, cols].bitcast(E4M3),
                scales=v_scales[g][:, cols],
                in_=pairs[g][:].rearrange("s b f t -> s (b f t)"),
            )

        def quantise_values(grouped, f, g):
            cols = slice(f * P, (f + 1) * P)
            nc.vector.quantize_mx(
                out=v_codes[g][:, cols].bitcast(E4M3),
                scales=v_scales[g][:, cols],
                in_=grouped[:].rearrange("s f t -> s (f t)"),
            )

        def group_weights(engine_copy, g, first, last):
            engine_copy(w_grouped[g][:, first:last, :], w_raw[g][:, :, first:last].rearrange("p j q -> p q j"))

        def quantise_weights(g, first, last):
            nc.vector.quantize_mx(
                out=w_codes[g][:, first:last].bitcast(E5M2),
                scales=w_scales[g][:, first:last],
                in_=w_grouped[g][:, first:last, :].rearrange("p q j -> p (q j)"),
            )

        def multiply(g, b):
            queries = slice(b * P, (b + 1) * P)
            nc.tensor.matmul_mx(
                out=sums[b][:],
                lhsT=w_codes[g][:, queries].bitcast(E5M2),
                lhsT_scale=w_scales[g][:, queries],
                rhs=v_codes[g][:].bitcast(E4M3),
                rhs_scale=v_scales[g][:],
                start=(g == 0),
                stop=(g == PASSES - 1),
            )

        def finish(engine_copy, result, b, first, last):
            engine_copy(result[:, first:last], sums[b][:, first:last])
            nc.sync.dma_start(out[0, b * P : (b + 1) * P, first:last], result[:, first:last])

        def gpsimd_copy(dst, src):
            nc.gpsimd.tensor_scalar(dst, src, 1.0, 0.0, mybir.AluOpType.mult, mybir.AluOpType.add)

        vector_copy = nc.vector.tensor_copy
        half3 = held.tile([P, TOKENS], BF16, name="half3")
        result0 = held.tile([P, FEATURES], F32, name="result0")
        result1 = held.tile([P, FEATURES], F32, name="result1")
        p10 = gather(vector_copy, pool_tiles[1], 0)
        p11 = gather(vector_copy, pool_tiles[1], 1)
        t10 = turn(p10)
        p20 = gather(vector_copy, pool_tiles[2], 0)
        t11 = turn(p11)
        empty_into(nc.scalar.copy, t10, pairs[0][:, 1])
        p21 = gather(vector_copy, pool_tiles[2], 1)
        t20 = turn(p20)
        empty_into(nc.scalar.copy, t11, pairs[1][:, 1])
        scalar_copy(half3[:, 1024:TOKENS], pool_tiles[3][:, 1024:TOKENS])
        vector_copy(half3[:, 0:1024], pool_tiles[3][:, 0:1024])
        t21 = turn(p21)
        p30 = gather(vector_copy, pool_tiles[3], 0)
        g20 = empty(nc.scalar.copy, t20)
        g21 = empty(nc.scalar.copy, t21)
        p00 = gather(vector_copy, pool_tiles[0], 0)
        t30 = turn(p30)
        p31 = gather(scalar_copy, half3, 1)
        quantise_values(g20, 2, 0)
        t00 = turn(p00)
        p01 = gather(vector_copy, pool_tiles[0], 1)
        g30 = empty(nc.scalar.copy, t30)
        group_weights(nc.scalar.copy, 0, 0, P)
        t31 = turn(p31)
        quantise_values(g21, 2, 1)
        empty_into(nc.scalar.copy, t00, pairs[0][:, 0])
        quantise_values(g30, 3, 0)
        quantise_weights(0, 0, P)
        group_weights(nc.scalar.copy, 0, P, QUERIES)
        t01 = turn(p01)
        quantise_pair(0)
        group_weights(nc.scalar.copy, 1, 0, P)
        quantise_weights(0, P, QUERIES)
        multiply(0, 0)
        empty_into(nc.scalar.copy, t01, pairs[1][:, 0])
        multiply(0, 1)
        quantise_weights(1, 0, P)
        g31 = empty(nc.scalar.copy, t31)
        quantise_pair(1)
        group_weights(nc.scalar.copy, 1, P, QUERIES)
        quantise_values(g31, 3, 1)
        multiply(1, 0)
        quantise_weights(1, P, QUERIES)
        finish(nc.scalar.copy, result0, 0, 0, FEATURES // 2)
        multiply(1, 1)
        finish(nc.scalar.copy, result0, 0, FEATURES // 2, FEATURES)
        finish(vector_copy, result1, 1, 0, FEATURES // 2)
        finish(vector_copy, result1, 1, FEATURES // 2, FEATURES)
